import numpy as np
import ml_dtypes


def mxq(x, axis, fmt="e4m3"):
    dtype, down = {"e4m3": (ml_dtypes.float8_e4m3fn, 7), "e5m2": (ml_dtypes.float8_e5m2, 14)}[fmt]
    v = np.moveaxis(np.asarray(x, np.float32).astype(ml_dtypes.bfloat16).astype(np.float64), axis, -1)
    blocks = v.reshape(v.shape[:-1] + (-1, 32))
    amax = np.abs(blocks).max(-1, keepdims=True)
    byte = np.maximum(np.where(amax > 0, np.frexp(amax)[1] - 1 + 127, 0) - down, 1)
    scale = np.exp2(byte - 127.0)
    codes = (blocks / scale).astype(np.float32).astype(dtype).astype(np.float64)
    return np.moveaxis((codes * scale).reshape(v.shape), -1, axis)


WIDE = False


def mx_kscale(k):
    if not WIDE:
        return np.ones(k)
    levels = np.array([10, -10, 5, -5, 0])
    if k % 512:
        return np.exp2(np.random.permutation(np.resize(levels, k // 32))).repeat(32)
    a = np.empty((k // 512, 16))
    for p in range(k // 512):
        a[p, :8] = np.random.permutation(np.resize(levels, 8))
        for g in range(8):
            far = levels[np.abs(levels - a[p, g]) >= 10]
            a[p, g + 8] = far[np.random.randint(len(far))]
    return np.exp2(a.ravel()).repeat(32)


def f64(x):
    return np.asarray(x).astype(np.float64)


def striped(idx):
    return np.tile(idx.reshape(-1, 16).T, (8, 1)).astype(np.uint16)


def unstriped(offs):
    return offs[:16].T.reshape(-1).astype(np.int64)


def silu(v):
    return v / (1.0 + np.exp(-np.maximum(v, -700.0)))


K, T, E, C, N = 1536, 1536, 4, 256, 128


def by_expert(wq, xq):
    return np.concatenate([wq[e].T @ xq[:, e * C:(e + 1) * C] for e in range(E)], axis=1)


def setup_inputs():
    n = np.random.standard_normal
    s = mx_kscale(K)[:, None]
    return {
        "xT": (n((K, T)) * s).astype(np.float32),
        "w": (n((E, K, N)) / np.sqrt(K) / s[None]).astype(np.float32),
        "b": (0.3 * n((N, E))).astype(np.float32),
        "gate": np.tile(np.random.uniform(0.2, 1.0, E * C), (K, 1)).astype(np.float32),
        "offs": striped(np.random.permutation(T)[:E * C]),
    }


def reference(xT, w, b, gate, offs):
    idx = unstriped(offs)
    xq = mxq(f64(gate) * f64(xT)[:, idx], 0, "e4m3")
    y = by_expert(mxq(f64(w), 1, "e4m3"), xq)
    y = silu(y + np.repeat(f64(b), C, axis=1))
    out = np.zeros((N, T))
    out[:, idx] = y
    return out

@@ -1,0 +1,178 @@
+from contextlib import ExitStack
+
+import concourse.mybir as mybir
+from concourse.masks import make_identity
+
+K, T, E, C, N = 1536, 1536, 4, 256, 128
+S = E * C
+FLOPS = 2 * K * N * S
+BYTES = 4 * (K * T + E * K * N + N * E + S + N * T) + 2 * 128 * (S // 16)
+
+F32 = mybir.dt.float32
+BF16 = mybir.dt.bfloat16
+U32 = mybir.dt.uint32
+U16 = mybir.dt.uint16
+U8 = mybir.dt.uint8
+FP8X4 = mybir.dt.float8_e4m3fn_x4
+ACT = mybir.ActivationFunctionType
+
+P = 128
+PACK = 4
+PASSES = K // (P * PACK)
+PER_COL = 16
+W_BEFORE = {(1, 0): 2, (1, 1): 1, (2, 0): 2, (2, 1): 1}
+PICK_BUFS = {1024: 4, 512: 6, 256: 12}
+UNITS = [[1, 1, 2], [2, 2], [1, 1, 1, 1]]
+
+
+def tile_moe_pre_lin_silu_kernel(tc, xT, w, b, gate, offs, out):
+    nc = tc.nc
+    with ExitStack() as ctx:
+        keep = ctx.enter_context(tc.tile_pool(name="keep", bufs=1))
+        ring = ctx.enter_context(tc.tile_pool(name="ring", bufs=4))
+        psum = ctx.enter_context(tc.psum_pool(name="psum", bufs=1))
+
+        offsets = keep.tile([P, S // PER_COL], U16, name="offsets")
+        nc.sync.dma_start(offsets[:], offs)
+
+        gate_rows = keep.tile([P, P], F32, name="gate_rows")
+        nc.vector.memset(gate_rows[:], 0.0)
+        nc.scalar.dma_start(gate_rows[0 : S // P, :], gate[0:1, :].rearrange("o (c q) -> (o c) q", q=P))
+        bias = keep.tile([P, E], F32, name="bias")
+        nc.scalar.dma_start(bias[:], b)
+
+        x_rows = xT.rearrange("(g p j) t -> g j p t", p=P, j=PACK)
+        w_rows = w.rearrange("e (g p j) n -> p (e g) j n", p=P, j=PACK)
+        x_plane = {}
+        w_raw = {}
+
+        def load_x(g, j):
+            x_plane[g, j] = keep.tile([P, T], F32, name="x_plane", tag="x_plane_%d_%d" % (g, j), align_bytes=64)
+            nc.sync.dma_start(x_plane[g, j][:], x_rows[g, j])
+
+        def load_w(i):
+            w_raw[i] = keep.tile([P, 2, PACK, N], F32, name="w_raw_%d" % i)
+            nc.sync.dma_start(w_raw[i][:], w_rows[:, 2 * i : 2 * i + 2])
+
+        pieces = 0
+        for g in range(PASSES):
+            for j in range(PACK):
+                for unused in range(W_BEFORE.get((g, j), 0)):
+                    load_w(pieces)
+                    pieces = pieces + 1
+                load_x(g, j)
+
+        ident = keep.tile([P, P], F32, name="ident")
+        make_identity(nc, ident[:])
+        result = keep.tile([P, T], F32, name="result")
+        nc.vector.memset(result[:, 8:T], 0.0)
+        nc.scalar.activation(result[:, 0:8], result[:, 8:16], ACT.Silu)
+
+        gate_bank = psum.tile([P, P], F32, name="gate_bank", tag="acc", bufs=2)
+        nc.tensor.transpose(gate_bank[:], gate_rows[:], ident[:])
+        gate_cols = keep.tile([P, S // P], F32, name="gate_cols")
+        nc.scalar.copy(gate_cols[:], gate_bank[:, 0 : S // P])
+
+        x_codes, x_scales, x_bf16, w_codes, w_scales, w_bf16 = {}, {}, {}, {}, {}, {}
+        for g in range(PASSES):
+            x_bf16[g] = keep.tile([P, S * PACK], BF16, name="x_bf16_%d" % g, align_bytes=64)
+            x_scales[g] = keep.tile([P, S], U8, name="x_scales_%d" % g, align_bytes=64)
+            w_bf16[g] = keep.tile([P, 4, N, PACK], BF16, name="w_bf16_%d" % g, align_bytes=64)
+            w_scales[g] = keep.tile([P, 4 * N], U8, name="w_scales_%d" % g, align_bytes=64)
+
+        def gather(g, j, first, count):
+            tile = ring.tile([P, count], F32, name="picked", tag="picked_%d" % count, bufs=PICK_BUFS[count])
+            cols = offsets[:, first // PER_COL : (first + count) // PER_COL]
+            nc.vector.tensor_copy(tile[:], x_plane[g, j][:].indirect(cols))
+            return (tile, first)
+
+        def weigh(g, e, picked):
+            back = psum.tile([P, 2, C], F32, name="back", bufs=2)
+            for h in range(C // P):
+                block = e * (C // P) + h
+                turned = psum.tile([P, PACK, P], F32, name="turned", bufs=4)
+                for j in range(PACK):
+                    tile, first = picked[j]
+                    lo = block * P - first
+                    nc.tensor.transpose(turned[:, j, :], tile[:, lo : lo + P], ident[:])
+                weighed = ring.tile([P, 2, P, 2], BF16, name="weighed")
+                nc.scalar.activation(
+                    weighed[:],
+                    turned[:].rearrange("s (u v) p -> s u p v", v=2),
+                    ACT.Copy,
+                    scale=gate_cols[:, block : block + 1],
+                )
+                words = weighed[:].rearrange("s u p v -> s (u p v)").bitcast(F32)
+                for u in range(2):
+                    nc.tensor.transpose(back[:, u, h * P : (h + 1) * P], words[:, u * P : (u + 1) * P], ident[:])
+            target = x_bf16[g][:, e * C * PACK : (e + 1) * C * PACK].bitcast(F32)
+            nc.scalar.copy(target.rearrange("p (s u) -> p s u", u=2), back[:].rearrange("p u s -> p s u"))
+
+        def quantize_x(g, first, count):
+            nc.vector.quantize_mx(
+                out=x_codes[g][:, first : first + count].bitcast(FP8X4),
+                scales=x_scales[g][:, first : first + count],
+                in_=x_bf16[g][:, first * PACK : (first + count) * PACK],
+            )
+
+        def cast_w(i):
+            half = w_bf16[i // 2][:, 2 * (i % 2) : 2 * (i % 2) + 2]
+            nc.scalar.copy(half, w_raw[i][:].rearrange("p e j n -> p e n j"))
+
+        def quantize_w(q, tag):
+            w_codes[q] = keep.tile([P, 4 * N], U32, name="w_codes", tag=tag, align_bytes=64)
+            nc.vector.quantize_mx(
+                out=w_codes[q][:].bitcast(FP8X4),
+                scales=w_scales[q][:],
+                in_=w_bf16[q][:].rearrange("p e n j -> p (e n j)"),
+            )
+
+        def multiply(e):
+            acc = psum.tile([P, C], F32, name="acc", tag="acc", bufs=2)
+            for g in range(PASSES):
+                q, r = divmod(e * PASSES + g, 4)
+                nc.tensor.matmul_mx(
+                    out=acc[:],
+                    lhsT=w_codes[q][:, r * N : (r + 1) * N].bitcast(FP8X4),
+                    lhsT_scale=w_scales[q][:, r * N : (r + 1) * N],
+                    rhs=x_codes[g][:, e * C : (e + 1) * C].bitcast(FP8X4),
+                    rhs_scale=x_scales[g][:, e * C : (e + 1) * C],
+                    start=(g == 0),
+                    stop=(g == PASSES - 1),
+                )
+            y = ring.tile([P, C], F32, name="y")
+            nc.scalar.activation(y[:], acc[:], ACT.Silu, bias=bias[:, e : e + 1])
+            return y
+
+        def scatter(e, y):
+            cols = offsets[:, e * C // PER_COL : (e + 1) * C // PER_COL]
+            nc.vector.tensor_copy(result[:].indirect(cols), y[:])
+
+        last = PASSES - 1
+        for g in range(PASSES):
+            whole = [gather(g, j, 0, S) for j in range(2)]
+            e0 = 0
+            parts = []
+            for experts in UNITS[g]:
+                part = [gather(g, j, e0 * C, experts * C) for j in range(2, PACK)]
+                parts.extend([part] * experts)
+                e0 = e0 + experts
+            if g > 0:
+                x_codes[g - 1] = keep.tile([P, S], U32, name="x_codes", tag="x_plane_%d_3" % g, align_bytes=64)
+                quantize_x(g - 1, 0, S)
+                cast_w(3 * g - 3)
+                cast_w(3 * g - 2)
+                if g == 1:
+                    quantize_w(0, "x_plane_1_2")
+                    cast_w(2)
+                else:
+                    quantize_w(1, "x_plane_2_2")
+                    cast_w(5)
+                    quantize_w(2, "x_plane_2_1")
+                    x_codes[last] = keep.tile([P, S], U32, name="x_codes_last", align_bytes=64)
+            for e in range(E):
+                weigh(g, e, whole + parts[e])
+                if g == last:
+                    quantize_x(last, e * C, C)
+                    scatter(e, multiply(e))
+        nc.sync.dma_start(out, result[:])

@@ -20,9 +20,9 @@ P = 128
 PACK = 4
 PASSES = K // (P * PACK)
 PER_COL = 16
-W_BEFORE = {(1, 0): 2, (1, 1): 1, (2, 0): 2, (2, 1): 1}
-PICK_BUFS = {1024: 4, 512: 6, 256: 12}
-UNITS = [[1, 1, 2], [2, 2], [1, 1, 1, 1]]
+W_BEFORE = {(1, 0): 2, (2, 0): 3, (2, 1): 1}
+LOADS = [(0, 1), (1, 1), (2, 2)]
+HALF = S // 2
 
 
 def tile_moe_pre_lin_silu_kernel(tc, xT, w, b, gate, offs, out):
@@ -36,19 +36,20 @@ def tile_moe_pre_lin_silu_kernel(tc, xT, w, b, gate, offs, out):
         nc.sync.dma_start(offsets[:], offs)
 
         gate_rows = keep.tile([P, P], F32, name="gate_rows")
-        nc.vector.memset(gate_rows[:], 0.0)
-        nc.scalar.dma_start(gate_rows[0 : S // P, :], gate[0:1, :].rearrange("o (c q) -> (o c) q", q=P))
+        nc.scalar.dma_start(gate_rows[:], gate[0 : P * P // S, :].rearrange("k (c q) -> (k c) q", q=P))
         bias = keep.tile([P, E], F32, name="bias")
         nc.scalar.dma_start(bias[:], b)
 
-        x_rows = xT.rearrange("(g p j) t -> g j p t", p=P, j=PACK)
+        x_rows = xT.rearrange("(g p j) t -> g p j t", p=P, j=PACK)
         w_rows = w.rearrange("e (g p j) n -> p (e g) j n", p=P, j=PACK)
         x_plane = {}
         w_raw = {}
 
-        def load_x(g, j):
-            x_plane[g, j] = keep.tile([P, T], F32, name="x_plane", tag="x_plane_%d_%d" % (g, j), align_bytes=64)
-            nc.sync.dma_start(x_plane[g, j][:], x_rows[g, j])
+        def load_x(g, j0, planes):
+            tile = keep.tile([P, planes * T], F32, name="x_planes", tag="x_planes_%d_%d" % (g, j0), align_bytes=64)
+            nc.sync.dma_start(tile[:], x_rows[g, :, j0 : j0 + planes].rearrange("p j t -> p (j t)"))
+            for j in range(planes):
+                x_plane[g, j0 + j] = tile[:, j * T : (j + 1) * T]
 
         def load_w(i):
             w_raw[i] = keep.tile([P, 2, PACK, N], F32, name="w_raw_%d" % i)
@@ -56,11 +57,11 @@ def tile_moe_pre_lin_silu_kernel(tc, xT, w, b, gate, offs, out):
 
         pieces = 0
         for g in range(PASSES):
-            for j in range(PACK):
-                for unused in range(W_BEFORE.get((g, j), 0)):
+            for j0, planes in LOADS:
+                for unused in range(W_BEFORE.get((g, j0), 0)):
                     load_w(pieces)
                     pieces = pieces + 1
-                load_x(g, j)
+                load_x(g, j0, planes)
 
         ident = keep.tile([P, P], F32, name="ident")
         make_identity(nc, ident[:])
@@ -81,9 +82,9 @@ def tile_moe_pre_lin_silu_kernel(tc, xT, w, b, gate, offs, out):
             w_scales[g] = keep.tile([P, 4 * N], U8, name="w_scales_%d" % g, align_bytes=64)
 
         def gather(g, j, first, count):
-            tile = ring.tile([P, count], F32, name="picked", tag="picked_%d" % count, bufs=PICK_BUFS[count])
+            tile = ring.tile([P, count], F32, name="picked", tag="picked_%d" % count, bufs=5 if count == S else 10)
             cols = offsets[:, first // PER_COL : (first + count) // PER_COL]
-            nc.vector.tensor_copy(tile[:], x_plane[g, j][:].indirect(cols))
+            nc.vector.tensor_copy(tile[:], x_plane[g, j].indirect(cols))
             return (tile, first)
 
         def weigh(g, e, picked):
@@ -108,6 +109,35 @@ def tile_moe_pre_lin_silu_kernel(tc, xT, w, b, gate, offs, out):
             target = x_bf16[g][:, e * C * PACK : (e + 1) * C * PACK].bitcast(F32)
             nc.scalar.copy(target.rearrange("p (s u) -> p s u", u=2), back[:].rearrange("p u s -> p s u"))
 
+        weighed_first = {}
+
+        def weigh_pair(e, u, picked):
+            turned = psum.tile([P, C // P, 2, P], F32, name="turned", bufs=4)
+            for h in range(C // P):
+                for v in range(2):
+                    tile, first = picked[v]
+                    lo = e * C + h * P - first
+                    nc.tensor.transpose(turned[:, h, v, :], tile[:, lo : lo + P], ident[:])
+            for h in range(C // P):
+                block = e * (C // P) + h
+                if u == 0:
+                    weighed_first[block] = keep.tile([P, 2, P, 2], BF16, name="weighed_first_%d" % block)
+                nc.scalar.activation(
+                    weighed_first[block][:, u],
+                    turned[:, h].rearrange("s v p -> s p v"),
+                    ACT.Copy,
+                    scale=gate_cols[:, block : block + 1],
+                )
+
+        def turn_back_first(e):
+            back = psum.tile([P, 2, C], F32, name="back", bufs=2)
+            for h in range(C // P):
+                words = weighed_first[e * (C // P) + h][:].rearrange("s u p v -> s (u p v)").bitcast(F32)
+                for u in range(2):
+                    nc.tensor.transpose(back[:, u, h * P : (h + 1) * P], words[:, u * P : (u + 1) * P], ident[:])
+            target = x_bf16[0][:, e * C * PACK : (e + 1) * C * PACK].bitcast(F32)
+            nc.scalar.copy(target.rearrange("p (s u) -> p s u", u=2), back[:].rearrange("p u s -> p s u"))
+
         def quantize_x(g, first, count):
             nc.vector.quantize_mx(
                 out=x_codes[g][:, first : first + count].bitcast(FP8X4),
@@ -117,12 +147,14 @@ def tile_moe_pre_lin_silu_kernel(tc, xT, w, b, gate, offs, out):
 
         def cast_w(i):
             half = w_bf16[i // 2][:, 2 * (i % 2) : 2 * (i % 2) + 2]
-            nc.scalar.copy(half, w_raw[i][:].rearrange("p e j n -> p e n j"))
+            nc.scalar.copy(
+                half.rearrange("p e (c i) j -> p e c j i", i=4),
+                w_raw[i][:].rearrange("p e j (c i) -> p e c j i", i=4),
+            )
 
-        def quantize_w(q, tag):
-            w_codes[q] = keep.tile([P, 4 * N], U32, name="w_codes", tag=tag, align_bytes=64)
+        def quantize_w(q):
             nc.vector.quantize_mx(
-                out=w_codes[q][:].bitcast(FP8X4),
+                out=w_codes[q].bitcast(FP8X4),
                 scales=w_scales[q][:],
                 in_=w_bf16[q][:].rearrange("p e n j -> p (e n j)"),
             )
@@ -149,30 +181,39 @@ def tile_moe_pre_lin_silu_kernel(tc, xT, w, b, gate, offs, out):
             nc.vector.tensor_copy(result[:].indirect(cols), y[:])
 
         last = PASSES - 1
-        for g in range(PASSES):
-            whole = [gather(g, j, 0, S) for j in range(2)]
-            e0 = 0
-            parts = []
-            for experts in UNITS[g]:
-                part = [gather(g, j, e0 * C, experts * C) for j in range(2, PACK)]
-                parts.extend([part] * experts)
-                e0 = e0 + experts
-            if g > 0:
-                x_codes[g - 1] = keep.tile([P, S], U32, name="x_codes", tag="x_plane_%d_3" % g, align_bytes=64)
-                quantize_x(g - 1, 0, S)
-                cast_w(3 * g - 3)
-                cast_w(3 * g - 2)
-                if g == 1:
-                    quantize_w(0, "x_plane_1_2")
-                    cast_w(2)
-                else:
-                    quantize_w(1, "x_plane_2_2")
-                    cast_w(5)
-                    quantize_w(2, "x_plane_2_1")
-                    x_codes[last] = keep.tile([P, S], U32, name="x_codes_last", align_bytes=64)
+        whole = gather(0, 0, 0, S)
+        for first in (0, HALF):
+            part = gather(0, 1, first, HALF)
+            for e in range(first // C, (first + HALF) // C):
+                weigh_pair(e, 0, [whole, part])
+        for first in (0, HALF):
+            parts = [gather(0, j, first, HALF) for j in (2, 3)]
+            for e in range(first // C, (first + HALF) // C):
+                weigh_pair(e, 1, parts)
+                turn_back_first(e)
+        cast_w(0)
+        cast_w(1)
+        for g in range(1, PASSES):
+            wholes = [gather(g, j, 0, S) for j in range(2)]
+            halves = [[gather(g, j, first, HALF) for j in (2, 3)] for first in (0, HALF)]
+            codes = keep.tile([P, S + g * 4 * N], U32, name="codes", tag="x_planes_%d_2" % g, align_bytes=64)
+            x_codes[g - 1] = codes[:, 0:S]
+            quantize_x(g - 1, 0, S)
+            for q in range(g - 1, 2 * g - 1):
+                w_codes[q] = codes[:, S + (q - g + 1) * 4 * N : S + (q - g + 2) * 4 * N]
+                quantize_w(q)
+            if g == last:
+                codes_last = keep.tile([P, S], U32, name="codes_last", align_bytes=64)
+                x_codes[last] = codes_last[:]
             for e in range(E):
-                weigh(g, e, whole + parts[e])
-                if g == last:
+                weigh(g, e, wholes + halves[e * C // HALF])
+                if g == last and e == 1:
+                    quantize_x(last, 0, HALF)
+                if g == last and e > 1:
                     quantize_x(last, e * C, C)
-                    scatter(e, multiply(e))
+            if g < last:
+                for i in range(2, 6):
+                    cast_w(i)
+        for e in range(E):
+            scatter(e, multiply(e))
         nc.sync.dma_start(out, result[:])

@@ -15,14 +15,21 @@ U16 = mybir.dt.uint16
 U8 = mybir.dt.uint8
 FP8X4 = mybir.dt.float8_e4m3fn_x4
 ACT = mybir.ActivationFunctionType
+ALU = mybir.AluOpType
 
 P = 128
 PACK = 4
 PASSES = K // (P * PACK)
-PER_COL = 16
-W_BEFORE = {(1, 0): 2, (2, 0): 3, (2, 1): 1}
-LOADS = [(0, 1), (1, 1), (2, 2)]
+LAST = PASSES - 1
+PER_COLUMN = 16
 HALF = S // 2
+BLOCKS = S // P
+MATRICES = E * PASSES
+PIECE = 2
+PIECES = MATRICES // PIECE
+EARLY_PIECES = 2
+FIRST_MATRICES = 8
+UNCUT = [3] * LAST + [2]
 
 
 def tile_moe_pre_lin_silu_kernel(tc, xT, w, b, gate, offs, out):
@@ -32,59 +39,64 @@ def tile_moe_pre_lin_silu_kernel(tc, xT, w, b, gate, offs, out):
         ring = ctx.enter_context(tc.tile_pool(name="ring", bufs=4))
         psum = ctx.enter_context(tc.psum_pool(name="psum", bufs=1))
 
-        offsets = keep.tile([P, S // PER_COL], U16, name="offsets")
+        offsets = keep.tile([P, S // PER_COLUMN], U16, name="offsets")
         nc.sync.dma_start(offsets[:], offs)
 
         gate_rows = keep.tile([P, P], F32, name="gate_rows")
-        nc.scalar.dma_start(gate_rows[:], gate[0 : P * P // S, :].rearrange("k (c q) -> (k c) q", q=P))
         bias = keep.tile([P, E], F32, name="bias")
-        nc.scalar.dma_start(bias[:], b)
-
         x_rows = xT.rearrange("(g p j) t -> g p j t", p=P, j=PACK)
         w_rows = w.rearrange("e (g p j) n -> p (e g) j n", p=P, j=PACK)
         x_plane = {}
         w_raw = {}
 
-        def load_x(g, j0, planes):
-            tile = keep.tile([P, planes * T], F32, name="x_planes", tag="x_planes_%d_%d" % (g, j0), align_bytes=64)
-            nc.sync.dma_start(tile[:], x_rows[g, :, j0 : j0 + planes].rearrange("p j t -> p (j t)"))
+        def load_x(g, first_j, planes):
+            tile = keep.tile([P, planes * T], F32, name="x_planes", tag="x_planes_%d_%d" % (g, first_j), align_bytes=64)
+            nc.sync.dma_start(tile[:], x_rows[g, :, first_j : first_j + planes].rearrange("p j t -> p (j t)"))
             for j in range(planes):
-                x_plane[g, j0 + j] = tile[:, j * T : (j + 1) * T]
+                x_plane[g, first_j + j] = tile[:, j * T : (j + 1) * T]
 
-        def load_w(i):
-            w_raw[i] = keep.tile([P, 2, PACK, N], F32, name="w_raw_%d" % i)
-            nc.sync.dma_start(w_raw[i][:], w_rows[:, 2 * i : 2 * i + 2])
+        def load_w(piece):
+            w_raw[piece] = keep.tile([P, PIECE, PACK, N], F32, name="w_raw_%d" % piece)
+            nc.sync.dma_start(w_raw[piece][:], w_rows[:, PIECE * piece : PIECE * (piece + 1)])
 
-        pieces = 0
         for g in range(PASSES):
-            for j0, planes in LOADS:
-                for unused in range(W_BEFORE.get((g, j0), 0)):
-                    load_w(pieces)
-                    pieces = pieces + 1
-                load_x(g, j0, planes)
+            if g == LAST:
+                for piece in range(EARLY_PIECES):
+                    load_w(piece)
+            for j in range(UNCUT[g]):
+                load_x(g, j, 1)
+                if (g, j) == (0, 1):
+                    nc.sync.dma_start(gate_rows[:], gate[0 : P // BLOCKS, :].rearrange("r (c q) -> (r c) q", q=P))
+            load_x(g, UNCUT[g], PACK - UNCUT[g])
+        for piece in range(EARLY_PIECES, PIECES):
+            load_w(piece)
+        nc.sync.dma_start(bias[:], b)
 
         ident = keep.tile([P, P], F32, name="ident")
         make_identity(nc, ident[:])
+
         result = keep.tile([P, T], F32, name="result")
         nc.vector.memset(result[:, 8:T], 0.0)
         nc.scalar.activation(result[:, 0:8], result[:, 8:16], ACT.Silu)
 
-        gate_bank = psum.tile([P, P], F32, name="gate_bank", tag="acc", bufs=2)
+        gate_bank = psum.tile([P, P], F32, name="gate_bank", tag="sums", bufs=2)
         nc.tensor.transpose(gate_bank[:], gate_rows[:], ident[:])
-        gate_cols = keep.tile([P, S // P], F32, name="gate_cols")
-        nc.scalar.copy(gate_cols[:], gate_bank[:, 0 : S // P])
+        gate_columns = keep.tile([P, BLOCKS], F32, name="gate_columns")
+        nc.scalar.copy(gate_columns[:], gate_bank[:, 0:BLOCKS])
 
-        x_codes, x_scales, x_bf16, w_codes, w_scales, w_bf16 = {}, {}, {}, {}, {}, {}
+        x_codes, x_scales, x_bf16, w_codes = {}, {}, {}, {}
         for g in range(PASSES):
             x_bf16[g] = keep.tile([P, S * PACK], BF16, name="x_bf16_%d" % g, align_bytes=64)
             x_scales[g] = keep.tile([P, S], U8, name="x_scales_%d" % g, align_bytes=64)
-            w_bf16[g] = keep.tile([P, 4, N, PACK], BF16, name="w_bf16_%d" % g, align_bytes=64)
-            w_scales[g] = keep.tile([P, 4 * N], U8, name="w_scales_%d" % g, align_bytes=64)
+        w_bf16 = keep.tile([P, MATRICES * N * PACK], BF16, name="w_bf16", align_bytes=64)
+        w_scales = keep.tile([P, MATRICES * N], U8, name="w_scales", align_bytes=64)
+
+        def list_columns(first, count):
+            return offsets[:, first // PER_COLUMN : (first + count) // PER_COLUMN]
 
         def gather(g, j, first, count):
-            tile = ring.tile([P, count], F32, name="picked", tag="picked_%d" % count, bufs=5 if count == S else 10)
-            cols = offsets[:, first // PER_COL : (first + count) // PER_COL]
-            nc.vector.tensor_copy(tile[:], x_plane[g, j].indirect(cols))
+            tile = ring.tile([P, count], F32, name="picked", tag="picked_%d" % count, bufs=8)
+            nc.vector.tensor_copy(tile[:], x_plane[g, j].indirect(list_columns(first, count)))
             return (tile, first)
 
         def weigh(g, e, picked):
@@ -94,48 +106,19 @@ def tile_moe_pre_lin_silu_kernel(tc, xT, w, b, gate, offs, out):
                 turned = psum.tile([P, PACK, P], F32, name="turned", bufs=4)
                 for j in range(PACK):
                     tile, first = picked[j]
-                    lo = block * P - first
-                    nc.tensor.transpose(turned[:, j, :], tile[:, lo : lo + P], ident[:])
+                    start = block * P - first
+                    nc.tensor.transpose(turned[:, j, :], tile[:, start : start + P], ident[:])
                 weighed = ring.tile([P, 2, P, 2], BF16, name="weighed")
                 nc.scalar.activation(
                     weighed[:],
                     turned[:].rearrange("s (u v) p -> s u p v", v=2),
                     ACT.Copy,
-                    scale=gate_cols[:, block : block + 1],
+                    scale=gate_columns[:, block : block + 1],
                 )
-                words = weighed[:].rearrange("s u p v -> s (u p v)").bitcast(F32)
+                pairs = weighed[:].rearrange("s u p v -> s (u p v)").bitcast(F32)
                 for u in range(2):
-                    nc.tensor.transpose(back[:, u, h * P : (h + 1) * P], words[:, u * P : (u + 1) * P], ident[:])
+                    nc.tensor.transpose(back[:, u, h * P : (h + 1) * P], pairs[:, u * P : (u + 1) * P], ident[:])
             target = x_bf16[g][:, e * C * PACK : (e + 1) * C * PACK].bitcast(F32)
-            nc.scalar.copy(target.rearrange("p (s u) -> p s u", u=2), back[:].rearrange("p u s -> p s u"))
-
-        weighed_first = {}
-
-        def weigh_pair(e, u, picked):
-            turned = psum.tile([P, C // P, 2, P], F32, name="turned", bufs=4)
-            for h in range(C // P):
-                for v in range(2):
-                    tile, first = picked[v]
-                    lo = e * C + h * P - first
-                    nc.tensor.transpose(turned[:, h, v, :], tile[:, lo : lo + P], ident[:])
-            for h in range(C // P):
-                block = e * (C // P) + h
-                if u == 0:
-                    weighed_first[block] = keep.tile([P, 2, P, 2], BF16, name="weighed_first_%d" % block)
-                nc.scalar.activation(
-                    weighed_first[block][:, u],
-                    turned[:, h].rearrange("s v p -> s p v"),
-                    ACT.Copy,
-                    scale=gate_cols[:, block : block + 1],
-                )
-
-        def turn_back_first(e):
-            back = psum.tile([P, 2, C], F32, name="back", bufs=2)
-            for h in range(C // P):
-                words = weighed_first[e * (C // P) + h][:].rearrange("s u p v -> s (u p v)").bitcast(F32)
-                for u in range(2):
-                    nc.tensor.transpose(back[:, u, h * P : (h + 1) * P], words[:, u * P : (u + 1) * P], ident[:])
-            target = x_bf16[0][:, e * C * PACK : (e + 1) * C * PACK].bitcast(F32)
             nc.scalar.copy(target.rearrange("p (s u) -> p s u", u=2), back[:].rearrange("p u s -> p s u"))
 
         def quantize_x(g, first, count):
@@ -145,75 +128,67 @@ def tile_moe_pre_lin_silu_kernel(tc, xT, w, b, gate, offs, out):
                 in_=x_bf16[g][:, first * PACK : (first + count) * PACK],
             )
 
-        def cast_w(i):
-            half = w_bf16[i // 2][:, 2 * (i % 2) : 2 * (i % 2) + 2]
-            nc.scalar.copy(
-                half.rearrange("p e (c i) j -> p e c j i", i=4),
-                w_raw[i][:].rearrange("p e j (c i) -> p e c j i", i=4),
+        def round_w(piece):
+            width = PIECE * N * PACK
+            target = w_bf16[:, piece * width : (piece + 1) * width].rearrange("p (m n j) -> p m n j", m=PIECE, j=PACK)
+            nc.gpsimd.tensor_scalar(target, w_raw[piece][:].rearrange("p m j n -> p m n j"), 1.0, 0.0, ALU.mult, ALU.add)
+
+        def quantize_w(first, count, codes):
+            for m in range(count):
+                w_codes[first + m] = codes[:, m * N : (m + 1) * N]
+            nc.vector.quantize_mx(
+                out=codes.bitcast(FP8X4),
+                scales=w_scales[:, first * N : (first + count) * N],
+                in_=w_bf16[:, first * N * PACK : (first + count) * N * PACK],
             )
 
-        def quantize_w(q):
-            nc.vector.quantize_mx(
-                out=w_codes[q].bitcast(FP8X4),
-                scales=w_scales[q][:],
-                in_=w_bf16[q][:].rearrange("p e n j -> p (e n j)"),
-            )
+        y = keep.tile([P, S], F32, name="y")
 
         def multiply(e):
-            acc = psum.tile([P, C], F32, name="acc", tag="acc", bufs=2)
+            sums = psum.tile([P, C], F32, name="sums", tag="sums", bufs=2)
             for g in range(PASSES):
-                q, r = divmod(e * PASSES + g, 4)
+                m = e * PASSES + g
                 nc.tensor.matmul_mx(
-                    out=acc[:],
-                    lhsT=w_codes[q][:, r * N : (r + 1) * N].bitcast(FP8X4),
-                    lhsT_scale=w_scales[q][:, r * N : (r + 1) * N],
+                    out=sums[:],
+                    lhsT=w_codes[m].bitcast(FP8X4),
+                    lhsT_scale=w_scales[:, m * N : (m + 1) * N],
                     rhs=x_codes[g][:, e * C : (e + 1) * C].bitcast(FP8X4),
                     rhs_scale=x_scales[g][:, e * C : (e + 1) * C],
                     start=(g == 0),
-                    stop=(g == PASSES - 1),
+                    stop=(g == LAST),
                 )
-            y = ring.tile([P, C], F32, name="y")
-            nc.scalar.activation(y[:], acc[:], ACT.Silu, bias=bias[:, e : e + 1])
-            return y
+            nc.scalar.activation(y[:, e * C : (e + 1) * C], sums[:], ACT.Silu, bias=bias[:, e : e + 1])
 
-        def scatter(e, y):
-            cols = offsets[:, e * C // PER_COL : (e + 1) * C // PER_COL]
-            nc.vector.tensor_copy(result[:].indirect(cols), y[:])
+        def scatter(first, count):
+            nc.vector.tensor_copy(result[:].indirect(list_columns(first, count)), y[:, first : first + count])
 
-        last = PASSES - 1
-        whole = gather(0, 0, 0, S)
-        for first in (0, HALF):
-            part = gather(0, 1, first, HALF)
-            for e in range(first // C, (first + HALF) // C):
-                weigh_pair(e, 0, [whole, part])
-        for first in (0, HALF):
-            parts = [gather(0, j, first, HALF) for j in (2, 3)]
-            for e in range(first // C, (first + HALF) // C):
-                weigh_pair(e, 1, parts)
-                turn_back_first(e)
-        cast_w(0)
-        cast_w(1)
-        for g in range(1, PASSES):
-            wholes = [gather(g, j, 0, S) for j in range(2)]
-            halves = [[gather(g, j, first, HALF) for j in (2, 3)] for first in (0, HALF)]
-            codes = keep.tile([P, S + g * 4 * N], U32, name="codes", tag="x_planes_%d_2" % g, align_bytes=64)
-            x_codes[g - 1] = codes[:, 0:S]
-            quantize_x(g - 1, 0, S)
-            for q in range(g - 1, 2 * g - 1):
-                w_codes[q] = codes[:, S + (q - g + 1) * 4 * N : S + (q - g + 2) * 4 * N]
-                quantize_w(q)
-            if g == last:
-                codes_last = keep.tile([P, S], U32, name="codes_last", align_bytes=64)
-                x_codes[last] = codes_last[:]
+        for piece in range(PIECES):
+            round_w(piece)
+
+        for g in range(PASSES):
+            uncut = [gather(g, j, 0, S) for j in range(UNCUT[g])]
+            halves = [[gather(g, j, first, HALF) for j in range(UNCUT[g], PACK)] for first in (0, HALF)]
+            if g == LAST:
+                codes = keep.tile(
+                    [P, LAST * S + FIRST_MATRICES * N], U32, name="codes", tag="x_planes_%d_%d" % (g, UNCUT[g]), align_bytes=64
+                )
+                codes_last = keep.tile([P, S + (MATRICES - FIRST_MATRICES) * N], U32, name="codes_last", align_bytes=64)
+                for earlier in range(LAST):
+                    x_codes[earlier] = codes[:, earlier * S : (earlier + 1) * S]
+                    quantize_x(earlier, 0, S)
+                quantize_w(0, FIRST_MATRICES, codes[:, LAST * S :])
+                x_codes[LAST] = codes_last[:, 0:S]
             for e in range(E):
-                weigh(g, e, wholes + halves[e * C // HALF])
-                if g == last and e == 1:
-                    quantize_x(last, 0, HALF)
-                if g == last and e > 1:
-                    quantize_x(last, e * C, C)
-            if g < last:
-                for i in range(2, 6):
-                    cast_w(i)
+                weigh(g, e, uncut + halves[e * C // HALF])
+                if g == LAST and (e + 1) * C == HALF:
+                    quantize_x(LAST, 0, HALF)
+                    quantize_w(FIRST_MATRICES, MATRICES - FIRST_MATRICES, codes_last[:, S:])
+                if g == LAST and e * C >= HALF:
+                    quantize_x(LAST, e * C, C)
+
         for e in range(E):
-            scatter(e, multiply(e))
+            multiply(e)
+        scatter(0, C)
+        scatter(C, (E - 2) * C)
+        scatter((E - 1) * C, C)
         nc.sync.dma_start(out, result[:])

from contextlib import ExitStack

import concourse.mybir as mybir
from concourse.masks import make_identity

K, T, E, C, N = 1536, 1536, 4, 256, 128
S = E * C
FLOPS = 2 * K * N * S
BYTES = 4 * (K * T + E * K * N + N * E + S + N * T) + 2 * 128 * (S // 16)

F32 = mybir.dt.float32
BF16 = mybir.dt.bfloat16
U32 = mybir.dt.uint32
U16 = mybir.dt.uint16
U8 = mybir.dt.uint8
FP8X4 = mybir.dt.float8_e4m3fn_x4
ACT = mybir.ActivationFunctionType
ALU = mybir.AluOpType

P = 128
PACK = 4
PASSES = K // (P * PACK)
LAST = PASSES - 1
PER_COLUMN = 16
HALF = S // 2
BLOCKS = S // P
MATRICES = E * PASSES
PIECE = 2
PIECES = MATRICES // PIECE
EARLY_PIECES = 2
FIRST_MATRICES = 8
UNCUT = [3] * LAST + [2]


def tile_moe_pre_lin_silu_kernel(tc, xT, w, b, gate, offs, out):
    nc = tc.nc
    with ExitStack() as ctx:
        keep = ctx.enter_context(tc.tile_pool(name="keep", bufs=1))
        ring = ctx.enter_context(tc.tile_pool(name="ring", bufs=4))
        psum = ctx.enter_context(tc.psum_pool(name="psum", bufs=1))

        offsets = keep.tile([P, S // PER_COLUMN], U16, name="offsets")
        nc.sync.dma_start(offsets[:], offs)

        gate_rows = keep.tile([P, P], F32, name="gate_rows")
        bias = keep.tile([P, E], F32, name="bias")
        x_rows = xT.rearrange("(g p j) t -> g p j t", p=P, j=PACK)
        w_rows = w.rearrange("e (g p j) n -> p (e g) j n", p=P, j=PACK)
        x_plane = {}
        w_raw = {}

        def load_x(g, first_j, planes):
            tile = keep.tile([P, planes * T], F32, name="x_planes", tag="x_planes_%d_%d" % (g, first_j), align_bytes=64)
            nc.sync.dma_start(tile[:], x_rows[g, :, first_j : first_j + planes].rearrange("p j t -> p (j t)"))
            for j in range(planes):
                x_plane[g, first_j + j] = tile[:, j * T : (j + 1) * T]

        def load_w(piece):
            w_raw[piece] = keep.tile([P, PIECE, PACK, N], F32, name="w_raw_%d" % piece)
            nc.sync.dma_start(w_raw[piece][:], w_rows[:, PIECE * piece : PIECE * (piece + 1)])

        for g in range(PASSES):
            if g == LAST:
                for piece in range(EARLY_PIECES):
                    load_w(piece)
            for j in range(UNCUT[g]):
                load_x(g, j, 1)
                if (g, j) == (0, 1):
                    nc.sync.dma_start(gate_rows[:], gate[0 : P // BLOCKS, :].rearrange("r (c q) -> (r c) q", q=P))
            load_x(g, UNCUT[g], PACK - UNCUT[g])
        for piece in range(EARLY_PIECES, PIECES):
            load_w(piece)
        nc.sync.dma_start(bias[:], b)

        ident = keep.tile([P, P], F32, name="ident")
        make_identity(nc, ident[:])

        result = keep.tile([P, T], F32, name="result")
        nc.vector.memset(result[:, 8:T], 0.0)
        nc.scalar.activation(result[:, 0:8], result[:, 8:16], ACT.Silu)

        gate_bank = psum.tile([P, P], F32, name="gate_bank", tag="sums", bufs=2)
        nc.tensor.transpose(gate_bank[:], gate_rows[:], ident[:])
        gate_columns = keep.tile([P, BLOCKS], F32, name="gate_columns")
        nc.scalar.copy(gate_columns[:], gate_bank[:, 0:BLOCKS])

        x_codes, x_scales, x_bf16, w_codes = {}, {}, {}, {}
        for g in range(PASSES):
            x_bf16[g] = keep.tile([P, S * PACK], BF16, name="x_bf16_%d" % g, align_bytes=64)
            x_scales[g] = keep.tile([P, S], U8, name="x_scales_%d" % g, align_bytes=64)
        w_bf16 = keep.tile([P, MATRICES * N * PACK], BF16, name="w_bf16", align_bytes=64)
        w_scales = keep.tile([P, MATRICES * N], U8, name="w_scales", align_bytes=64)

        def list_columns(first, count):
            return offsets[:, first // PER_COLUMN : (first + count) // PER_COLUMN]

        def gather(g, j, first, count):
            tile = ring.tile([P, count], F32, name="picked", tag="picked_%d" % count, bufs=8)
            nc.vector.tensor_copy(tile[:], x_plane[g, j].indirect(list_columns(first, count)))
            return (tile, first)

        def weigh(g, e, picked):
            back = psum.tile([P, 2, C], F32, name="back", bufs=2)
            for h in range(C // P):
                block = e * (C // P) + h
                turned = psum.tile([P, PACK, P], F32, name="turned", bufs=4)
                for j in range(PACK):
                    tile, first = picked[j]
                    start = block * P - first
                    nc.tensor.transpose(turned[:, j, :], tile[:, start : start + P], ident[:])
                weighed = ring.tile([P, 2, P, 2], BF16, name="weighed")
                nc.scalar.activation(
                    weighed[:],
                    turned[:].rearrange("s (u v) p -> s u p v", v=2),
                    ACT.Copy,
                    scale=gate_columns[:, block : block + 1],
                )
                pairs = weighed[:].rearrange("s u p v -> s (u p v)").bitcast(F32)
                for u in range(2):
                    nc.tensor.transpose(back[:, u, h * P : (h + 1) * P], pairs[:, u * P : (u + 1) * P], ident[:])
            target = x_bf16[g][:, e * C * PACK : (e + 1) * C * PACK].bitcast(F32)
            nc.scalar.copy(target.rearrange("p (s u) -> p s u", u=2), back[:].rearrange("p u s -> p s u"))

        def quantize_x(g, first, count):
            nc.vector.quantize_mx(
                out=x_codes[g][:, first : first + count].bitcast(FP8X4),
                scales=x_scales[g][:, first : first + count],
                in_=x_bf16[g][:, first * PACK : (first + count) * PACK],
            )

        def round_w(piece):
            width = PIECE * N * PACK
            target = w_bf16[:, piece * width : (piece + 1) * width].rearrange("p (m n j) -> p m n j", m=PIECE, j=PACK)
            nc.gpsimd.tensor_scalar(target, w_raw[piece][:].rearrange("p m j n -> p m n j"), 1.0, 0.0, ALU.mult, ALU.add)

        def quantize_w(first, count, codes):
            for m in range(count):
                w_codes[first + m] = codes[:, m * N : (m + 1) * N]
            nc.vector.quantize_mx(
                out=codes.bitcast(FP8X4),
                scales=w_scales[:, first * N : (first + count) * N],
                in_=w_bf16[:, first * N * PACK : (first + count) * N * PACK],
            )

        y = keep.tile([P, S], F32, name="y")

        def multiply(e):
            sums = psum.tile([P, C], F32, name="sums", tag="sums", bufs=2)
            for g in range(PASSES):
                m = e * PASSES + g
                nc.tensor.matmul_mx(
                    out=sums[:],
                    lhsT=w_codes[m].bitcast(FP8X4),
                    lhsT_scale=w_scales[:, m * N : (m + 1) * N],
                    rhs=x_codes[g][:, e * C : (e + 1) * C].bitcast(FP8X4),
                    rhs_scale=x_scales[g][:, e * C : (e + 1) * C],
                    start=(g == 0),
                    stop=(g == LAST),
                )
            nc.scalar.activation(y[:, e * C : (e + 1) * C], sums[:], ACT.Silu, bias=bias[:, e : e + 1])

        def scatter(first, count):
            nc.vector.tensor_copy(result[:].indirect(list_columns(first, count)), y[:, first : first + count])

        for piece in range(PIECES):
            round_w(piece)

        for g in range(PASSES):
            uncut = [gather(g, j, 0, S) for j in range(UNCUT[g])]
            halves = [[gather(g, j, first, HALF) for j in range(UNCUT[g], PACK)] for first in (0, HALF)]
            if g == LAST:
                codes = keep.tile(
                    [P, LAST * S + FIRST_MATRICES * N], U32, name="codes", tag="x_planes_%d_%d" % (g, UNCUT[g]), align_bytes=64
                )
                codes_last = keep.tile([P, S + (MATRICES - FIRST_MATRICES) * N], U32, name="codes_last", align_bytes=64)
                for earlier in range(LAST):
                    x_codes[earlier] = codes[:, earlier * S : (earlier + 1) * S]
                    quantize_x(earlier, 0, S)
                quantize_w(0, FIRST_MATRICES, codes[:, LAST * S :])
                x_codes[LAST] = codes_last[:, 0:S]
            for e in range(E):
                weigh(g, e, uncut + halves[e * C // HALF])
                if g == LAST and (e + 1) * C == HALF:
                    quantize_x(LAST, 0, HALF)
                    quantize_w(FIRST_MATRICES, MATRICES - FIRST_MATRICES, codes_last[:, S:])
                if g == LAST and e * C >= HALF:
                    quantize_x(LAST, e * C, C)

        for e in range(E):
            multiply(e)
        scatter(0, C)
        scatter(C, (E - 2) * C)
        scatter((E - 1) * C, C)
        nc.sync.dma_start(out, result[:])
